import numpy as np
import ml_dtypes

BF16 = ml_dtypes.bfloat16


def bf(x):
    return np.asarray(x, np.float32).astype(BF16)


def f32(x):
    return np.asarray(x, np.float32)


def f64(x):
    return np.asarray(x).astype(np.float64)


def striped(idx):
    return np.tile(idx.reshape(-1, 16).T, (8, 1))


def rows(idx, k):
    return np.tile(idx, (k, 1))


def look(tab, idx):
    return np.take_along_axis(f64(tab), rows(idx, len(tab)), axis=1)


K, S, D, V, N = 512, 2048, 3, 512, 1536


def setup_inputs():
    return {"tab": bf(np.random.standard_normal((K, S))), "u": bf(np.random.uniform(0.2, 1.0, (D, K, V))), "offs": striped(np.random.permutation(S)[:N])}


def reference(tab, u, offs):
    idx = offs[:16].T.reshape(-1)
    x = sum(f64(u[d]) * look(tab, idx[d * V:(d + 1) * V]) for d in range(D))
    return x

@@ -1,0 +1,43 @@
+import concourse.mybir as mybir
+from concourse.masks import make_identity
+
+P = 128
+BF16, F32, U16 = mybir.dt.bfloat16, mybir.dt.float32, mybir.dt.uint16
+MULT = mybir.AluOpType.mult
+
+
+def tile_lookup_mix_mul_out_kernel(tc, tab, u, offs, out):
+    nc = tc.nc
+    rows, table_columns = tab.shape
+    pieces, width = u.shape[0], u.shape[2]
+    blocks = rows // P
+    list_columns = width // 16
+
+    with (
+        tc.tile_pool(name="held", bufs=1) as held,
+        tc.tile_pool(name="loads", bufs=blocks) as loads,
+        tc.tile_pool(name="work", bufs=4) as work,
+        tc.psum_pool(name="sums", bufs=2) as sums,
+    ):
+        offsets = held.tile([P, pieces * list_columns], U16, name="offsets")
+        nc.sync.dma_start(offsets[:], offs)
+        identity = held.tile([P, P], BF16, name="identity")
+        make_identity(nc, identity[:])
+
+        for b in range(blocks):
+            block_rows = slice(b * P, (b + 1) * P)
+            table = loads.tile([P, table_columns], BF16, name="table")
+            nc.sync.dma_start(table[:], tab[block_rows, :])
+            weights = loads.tile([P, pieces, width], BF16, name="weights")
+            nc.sync.dma_start(weights[:], u[:, block_rows, :].rearrange("d p v -> p d v"))
+
+            total = sums.tile([P, width], F32, name="total")
+            for d in range(pieces):
+                piece = offsets[:, d * list_columns : (d + 1) * list_columns]
+                product = work.tile([P, width], BF16, name="product")
+                nc.vector.tensor_tensor(product[:], table[:].indirect(piece), weights[:, d, :], MULT)
+                nc.tensor.matmul(total[:], identity[:], product[:], start=d == 0, stop=d == pieces - 1)
+
+            result = work.tile([P, width], F32, name="result")
+            nc.scalar.copy(result[:], total[:])
+            nc.scalar.dma_start(out[block_rows, :], result[:])

@@ -3,7 +3,7 @@ from concourse.masks import make_identity
 
 P = 128
 BF16, F32, U16 = mybir.dt.bfloat16, mybir.dt.float32, mybir.dt.uint16
-MULT = mybir.AluOpType.mult
+MULT, ADD = mybir.AluOpType.mult, mybir.AluOpType.add
 
 
 def tile_lookup_mix_mul_out_kernel(tc, tab, u, offs, out):
@@ -11,6 +11,7 @@ def tile_lookup_mix_mul_out_kernel(tc, tab, u, offs, out):
     rows, table_columns = tab.shape
     pieces, width = u.shape[0], u.shape[2]
     blocks = rows // P
+    half = width // 2
     list_columns = width // 16
 
     with (
@@ -28,16 +29,30 @@ def tile_lookup_mix_mul_out_kernel(tc, tab, u, offs, out):
             block_rows = slice(b * P, (b + 1) * P)
             table = loads.tile([P, table_columns], BF16, name="table")
             nc.sync.dma_start(table[:], tab[block_rows, :])
-            weights = loads.tile([P, pieces, width], BF16, name="weights")
-            nc.sync.dma_start(weights[:], u[:, block_rows, :].rearrange("d p v -> p d v"))
+            weights = []
+            for d in range(pieces):
+                weight = loads.tile([P, width], BF16, name=f"weight{d}")
+                nc.sync.dma_start(weight[:], u[d, block_rows, :])
+                weights.append(weight)
 
-            total = sums.tile([P, width], F32, name="total")
+            last_block = b == blocks - 1
+            summed_on_tensor = pieces - 1 if last_block else pieces
+            totals = [sums.tile([P, half], F32, name=f"total{h}") for h in range(2)]
             for d in range(pieces):
                 piece = offsets[:, d * list_columns : (d + 1) * list_columns]
                 product = work.tile([P, width], BF16, name="product")
-                nc.vector.tensor_tensor(product[:], table[:].indirect(piece), weights[:, d, :], MULT)
-                nc.tensor.matmul(total[:], identity[:], product[:], start=d == 0, stop=d == pieces - 1)
+                nc.vector.tensor_tensor(product[:], table[:].indirect(piece), weights[d][:], MULT)
+                if d < summed_on_tensor:
+                    for h in range(2):
+                        columns = slice(h * half, (h + 1) * half)
+                        nc.tensor.matmul(totals[h][:], identity[:], product[:, columns], start=d == 0, stop=d == summed_on_tensor - 1)
 
-            result = work.tile([P, width], F32, name="result")
-            nc.scalar.copy(result[:], total[:])
-            nc.scalar.dma_start(out[block_rows, :], result[:])
+            for h in range(2):
+                columns = slice(h * half, (h + 1) * half)
+                result = work.tile([P, half], F32, name=f"result{h}")
+                if last_block:
+                    nc.vector.tensor_tensor(result[:], totals[h][:], product[:, columns], ADD)
+                else:
+                    nc.scalar.copy(result[:], totals[h][:])
+                queue = nc.scalar if h == 0 else nc.sync
+                queue.dma_start(out[block_rows, columns], result[:])

import concourse.mybir as mybir
from concourse.masks import make_identity

P = 128
BF16, F32, U16 = mybir.dt.bfloat16, mybir.dt.float32, mybir.dt.uint16
MULT, ADD = mybir.AluOpType.mult, mybir.AluOpType.add


def tile_lookup_mix_mul_out_kernel(tc, tab, u, offs, out):
    nc = tc.nc
    rows, table_columns = tab.shape
    pieces, width = u.shape[0], u.shape[2]
    blocks = rows // P
    half = width // 2
    list_columns = width // 16

    with (
        tc.tile_pool(name="held", bufs=1) as held,
        tc.tile_pool(name="loads", bufs=blocks) as loads,
        tc.tile_pool(name="work", bufs=4) as work,
        tc.psum_pool(name="sums", bufs=2) as sums,
    ):
        offsets = held.tile([P, pieces * list_columns], U16, name="offsets")
        nc.sync.dma_start(offsets[:], offs)
        identity = held.tile([P, P], BF16, name="identity")
        make_identity(nc, identity[:])

        for b in range(blocks):
            block_rows = slice(b * P, (b + 1) * P)
            table = loads.tile([P, table_columns], BF16, name="table")
            nc.sync.dma_start(table[:], tab[block_rows, :])
            weights = []
            for d in range(pieces):
                weight = loads.tile([P, width], BF16, name=f"weight{d}")
                nc.sync.dma_start(weight[:], u[d, block_rows, :])
                weights.append(weight)

            last_block = b == blocks - 1
            summed_on_tensor = pieces - 1 if last_block else pieces
            totals = [sums.tile([P, half], F32, name=f"total{h}") for h in range(2)]
            for d in range(pieces):
                piece = offsets[:, d * list_columns : (d + 1) * list_columns]
                product = work.tile([P, width], BF16, name="product")
                nc.vector.tensor_tensor(product[:], table[:].indirect(piece), weights[d][:], MULT)
                if d < summed_on_tensor:
                    for h in range(2):
                        columns = slice(h * half, (h + 1) * half)
                        nc.tensor.matmul(totals[h][:], identity[:], product[:, columns], start=d == 0, stop=d == summed_on_tensor - 1)

            for h in range(2):
                columns = slice(h * half, (h + 1) * half)
                result = work.tile([P, half], F32, name=f"result{h}")
                if last_block:
                    nc.vector.tensor_tensor(result[:], totals[h][:], product[:, columns], ADD)
                else:
                    nc.scalar.copy(result[:], totals[h][:])
                queue = nc.scalar if h == 0 else nc.sync
                queue.dma_start(out[block_rows, columns], result[:])
